import numpy as np
import ml_dtypes


def mxq(x, axis, fmt="e4m3"):
    dtype, down = {"e4m3": (ml_dtypes.float8_e4m3fn, 7), "e5m2": (ml_dtypes.float8_e5m2, 14)}[fmt]
    v = np.moveaxis(np.asarray(x, np.float32).astype(ml_dtypes.bfloat16).astype(np.float64), axis, -1)
    blocks = v.reshape(v.shape[:-1] + (-1, 32))
    amax = np.abs(blocks).max(-1, keepdims=True)
    byte = np.maximum(np.where(amax > 0, np.frexp(amax)[1] - 1 + 127, 0) - down, 1)
    scale = np.exp2(byte - 127.0)
    codes = (blocks / scale).astype(np.float32).astype(dtype).astype(np.float64)
    return np.moveaxis((codes * scale).reshape(v.shape), -1, axis)


WIDE = False


def mx_kscale(k):
    if not WIDE:
        return np.ones(k)
    levels = np.array([18, -18])
    if k % 512:
        return np.exp2(np.random.permutation(np.resize(levels, k // 32))).repeat(32)
    a = np.empty((k // 512, 16))
    for p in range(k // 512):
        a[p, :8] = np.random.permutation(np.resize(levels, 8))
        for g in range(8):
            far = levels[np.abs(levels - a[p, g]) >= 10]
            a[p, g + 8] = far[np.random.randint(len(far))]
    return np.exp2(a.ravel()).repeat(32)


def f64(x):
    return np.asarray(x).astype(np.float64)


def striped(idx):
    return np.tile(np.asarray(idx).reshape(-1, 16).T, (8, 1)).astype(np.uint16)


def unstriped(offs):
    return offs[:16].T.reshape(-1).astype(np.int64)

def planes(y):
    n, m = y.shape
    v = y.astype(np.float32).astype(ml_dtypes.bfloat16).astype(np.float64).reshape(n // 32, 32, m)
    top = np.abs(v).max(1)
    byte = np.clip(np.where(top > 0, np.frexp(top)[1] - 1 + 127 - 7, 1), 1, 254)
    codes = (v * np.exp2(127.0 - byte)[:, None, :]).reshape(n, m).astype(np.float32).astype(ml_dtypes.float8_e4m3fn).view(np.uint8)
    words = codes.reshape(n // 512, 128, 4, m).transpose(0, 1, 3, 2)
    return np.ascontiguousarray(words), np.ascontiguousarray(byte.astype(np.uint8).reshape(n // 512, 16, m))


B, N, T, D, R = 1, 512, 2048, 512, 512
LR = 0.1
BETA = 0.9


def setup_inputs():
    n = np.random.standard_normal
    idx = np.random.permutation(T)[:B * N]
    s = mx_kscale(D)[:, None]
    z = mx_kscale(R)[:, None]
    x = n((B, D, R))
    return {
        "xT": (x * s).astype(np.float32),
        "wT": (n((D, T)) * (1.00 / np.sqrt(D)) / s).astype(np.float32),
        "y": n((B, R, N)).astype(np.float32),
        "wt": (np.random.uniform(0.5, 1.5, (B, R, 1)) * 1.0 / np.sqrt(R) * z).astype(np.float32),
        "xm": (x.transpose(0, 2, 1) / z / s[:, 0]).astype(np.float32),
        "mT": (0.3 * n((D, T)) / s).astype(np.float32),
        "offs": striped(idx),
    }


def reference(xT, wT, y, wt, xm, mT, offs):
    idx = unstriped(offs)
    pick = lambda x: x[:, idx].reshape(x.shape[0], B, N).transpose(1, 0, 2)
    w = pick(f64(wT))
    a = mxq(f64(xT), 1, "e4m3").transpose(0, 2, 1) @ mxq(w, 1, "e4m3")
    g = f64(wt) * np.tanh(a - f64(y))
    dw = mxq(f64(xm), 1, "e4m3").transpose(0, 2, 1) @ mxq(g, 1, "e5m2")
    nm = BETA * pick(f64(mT)) + dw
    nw = w - LR * (dw + BETA * nm)
    tables = []
    for old, new in ((wT, nw), (mT, nm),):
        table = f64(old)
        table[:, idx] = new.transpose(1, 0, 2).reshape(D, B * N)
        tables.append(table)
    return tuple(tables) + planes(tables[0])

@@ -1,0 +1,234 @@
+from contextlib import ExitStack
+
+import concourse.mybir as mybir
+
+D, R, N, T = 512, 512, 512, 2048
+LR, BETA = 0.1, 0.9
+FLOPS = 2 * 2 * D * R * N
+
+F32 = mybir.dt.float32
+BF16 = mybir.dt.bfloat16
+I32 = mybir.dt.int32
+U32 = mybir.dt.uint32
+U16 = mybir.dt.uint16
+U8 = mybir.dt.uint8
+E4M3 = mybir.dt.float8_e4m3fn_x4
+E5M2 = mybir.dt.float8_e5m2_x4
+COPY = mybir.ActivationFunctionType.Copy
+TANH = mybir.ActivationFunctionType.Tanh
+MULT = mybir.AluOpType.mult
+ADD = mybir.AluOpType.add
+SUB = mybir.AluOpType.subtract
+
+P = 128
+PACK = 4
+M_IN_W = -LR * BETA * BETA
+DW_IN_W = -LR * (1.0 + BETA)
+
+
+def tile_attend_glch_pl_nag_kernel(tc, xT, wT, y, wt, xm, mT, offs, out_0, out_1, out_2, out_3):
+    nc = tc.nc
+    with ExitStack() as ctx:
+        keep = ctx.enter_context(tc.tile_pool(name="keep", bufs=1))
+        woven = ctx.enter_context(tc.tile_pool(name="woven", bufs=5))
+        psum = ctx.enter_context(tc.psum_pool(name="psum", bufs=1))
+
+        def planes_of(table):
+            return table.rearrange("(p t) c -> t p c", t=PACK)
+
+        offsets = keep.tile([P, N // 16], U16, name="offsets")
+        w_src = [keep.tile([P, T], F32, name="w_src%d" % t) for t in range(PACK)]
+        w_dst = [keep.tile([P, T], F32, name="w_dst%d" % t) for t in range(PACK)]
+        m_src = [keep.tile([P, T], F32, name="m_src%d" % t) for t in range(PACK)]
+        m_dst = [keep.tile([P, T], F32, name="m_dst%d" % t) for t in range(PACK)]
+        x_raw = keep.tile([P, PACK, R], F32, name="x_raw")
+        xm_raw = keep.tile([P, PACK, D], F32, name="xm_raw")
+        y_sb = [keep.tile([P, N], F32, name="y%d" % t, tag="ym%d" % t) for t in range(PACK)]
+        wt_sb = keep.tile([P, PACK], F32, name="wt_sb")
+        w_got = keep.tile([P, PACK, N], F32, name="w_got", tag="wm")
+        m_got = [keep.tile([P, N], F32, name="m_got%d" % t) for t in range(PACK)]
+        resid = [keep.tile([P, N], F32, name="resid%d" % t, tag="rw%d" % t) for t in range(PACK)]
+
+        def codes_and_scales(name, width):
+            return (keep.tile([P, width], U32, name=name + "_codes", align_bytes=64),
+                    keep.tile([P, width], U8, name=name + "_scales", align_bytes=64))
+
+        x_q = codes_and_scales("x", R)
+        w_q = codes_and_scales("w", N)
+        xm_q = codes_and_scales("xm", D)
+        g_q = codes_and_scales("g", N)
+        o_q = codes_and_scales("o", T)
+
+        def stage(name):
+            return woven.tile([P, PACK * 512], BF16, name=name, tag="woven", align_bytes=64)
+
+        def quantize(q, src, fmt, cols=slice(None)):
+            nc.vector.quantize_mx(out=q[0][:, cols].bitcast(fmt), scales=q[1][:, cols], in_=src)
+
+        def deal(raw, dst):
+            out_v = dst[:].rearrange("p (t m j) -> p m j t", t=PACK, j=PACK)
+            in_v = raw[:].rearrange("p j (m t) -> p m j t", t=PACK)
+            nc.scalar.activation(out_v[:, :P // 2], in_v[:, :P // 2], COPY)
+            nc.vector.tensor_copy(out_v[:, P // 2:], in_v[:, P // 2:])
+
+        def weave_views(dst, src):
+            return (dst.rearrange("p (c i t) -> p c t i", i=4, t=PACK),
+                    src.rearrange("p t (c i) -> p c t i", i=4))
+
+        nc.sync.dma_start(offsets[:], offs)
+        for t in range(PACK):
+            nc.sync.dma_start(w_src[t][:], planes_of(wT)[t])
+        nc.sync.dma_start(x_raw[:], xT[0].rearrange("(p j) r -> p j r", j=PACK))
+        nc.sync.dma_start(xm_raw[:], xm[0].rearrange("(p j) d -> p j d", j=PACK))
+        for r in range(PACK):
+            nc.sync.dma_start(y_sb[r][:], planes_of(y[0])[r])
+        nc.sync.dma_start(wt_sb[:], wt[0].rearrange("(p j) o -> p (j o)", j=PACK))
+        for t in range(PACK):
+            nc.sync.dma_start(m_src[t][:], planes_of(mT)[t])
+        for t in (1, 3):
+            nc.sync.dma_start(m_dst[t][:], planes_of(mT)[t])
+
+        def gather_w(t):
+            nc.vector.tensor_copy(w_got[:, t, :], w_src[t][:].indirect(offsets[:]))
+            nc.scalar.activation(w_dst[t][:], w_src[t][:], COPY)
+
+        def gather_m(t):
+            nc.scalar.activation(m_got[t][:], m_src[t][:].indirect(offsets[:]), COPY, scale=M_IN_W)
+
+        for t in range(PACK):
+            gather_w(t)
+        w_w = stage("w_w")
+        nc.vector.tensor_copy(*weave_views(w_w[:], w_got[:]))
+        quantize(w_q, w_w[:], E4M3)
+        x_w = stage("x_w")
+        deal(x_raw, x_w)
+        quantize(x_q, x_w[:], E4M3)
+        xm_w = stage("xm_w")
+        deal(xm_raw, xm_w)
+
+        for r in range(PACK):
+            score = psum.tile([P, N], F32, name="score%d" % r)
+            cols = slice(r * P, (r + 1) * P)
+            nc.tensor.matmul_mx(out=score[:], lhsT=x_q[0][:, cols].bitcast(E4M3), lhsT_scale=x_q[1][:, cols],
+                                rhs=w_q[0][:].bitcast(E4M3), rhs_scale=w_q[1][:], start=True, stop=True)
+            nc.vector.tensor_tensor(resid[r][:], score[:], y_sb[r][:], SUB)
+            nc.scalar.activation(resid[r][:], resid[r][:], TANH)
+        g_pairs = stage("g_pairs")
+        g_half = g_pairs[:].rearrange("p (u i e) -> p u i e", u=2, e=2)
+        for r in range(PACK):
+            nc.vector.tensor_scalar(g_half[:, r // 2, :, r % 2], resid[r][:], wt_sb[:, r:r + 1], None, MULT)
+        g_w = stage("g_w")
+        nc.vector.tensor_copy(g_w[:].bitcast(F32).rearrange("p (i u) -> p i u", u=2),
+                              g_pairs[:].bitcast(F32).rearrange("p (u i) -> p i u", u=2))
+        quantize(xm_q, xm_w[:, :PACK * P], E4M3, slice(0, P))
+        quantize(g_q, g_w[:], E5M2)
+        for t in range(1, PACK):
+            quantize(xm_q, xm_w[:, t * PACK * P:(t + 1) * PACK * P], E4M3, slice(t * P, (t + 1) * P))
+
+        gather_m(0)
+        nc.scalar.activation(m_dst[0][:, :T // 2], m_src[0][:, :T // 2], COPY)
+        gather_m(1)
+
+        dw = []
+        for t in range(PACK):
+            bank = psum.tile([P, N], F32, name="dw%d" % t)
+            cols = slice(t * P, (t + 1) * P)
+            nc.tensor.matmul_mx(out=bank[:], lhsT=xm_q[0][:, cols].bitcast(E4M3), lhsT_scale=xm_q[1][:, cols],
+                                rhs=g_q[0][:].bitcast(E5M2), rhs_scale=g_q[1][:], start=True, stop=True)
+            dw.append(bank)
+
+        w_part = [keep.tile([P, N], F32, name="w_part%d" % t, tag="rw%d" % t) for t in range(PACK)]
+        m_new = [keep.tile([P, N], F32, name="m_new%d" % t, tag="ym%d" % t if t else "wm") for t in range(PACK)]
+
+        def scatter_on_scalar(window, values):
+            for h in range(2):
+                nc.scalar.activation(window[:].indirect(offsets[:, 16 * h:16 * (h + 1)]),
+                                     values[:, 256 * h:256 * (h + 1)], COPY)
+
+        def w_for_scalar(t):
+            nc.vector.tensor_tensor(w_part[t][:], w_got[:, t, :], m_got[t][:], ADD)
+            nc.vector.scalar_tensor_tensor(w_part[t][:], dw[t][:], DW_IN_W, w_part[t][:], MULT, ADD)
+
+        def w_on_scalar(t):
+            scatter_on_scalar(w_dst[t], w_part[t])
+            nc.sync.dma_start(planes_of(out_0)[t], w_dst[t][:])
+
+        def w_for_vector(t):
+            nc.vector.scalar_tensor_tensor(w_part[t][:], dw[t][:], DW_IN_W, w_got[:, t, :], MULT, ADD)
+
+        def w_on_vector(t):
+            nc.vector.tensor_tensor(w_dst[t][:].indirect(offsets[:]), w_part[t][:], m_got[t][:], ADD)
+            nc.sync.dma_start(planes_of(out_0)[t], w_dst[t][:])
+
+        def m_sum(t):
+            nc.vector.scalar_tensor_tensor(m_new[t][:], m_got[t][:], BETA / M_IN_W, dw[t][:], MULT, ADD)
+
+        def m_on_scalar(t):
+            scatter_on_scalar(m_dst[t], m_new[t])
+            queue = nc.scalar if t == PACK - 1 else nc.sync
+            queue.dma_start(planes_of(out_1)[t], m_dst[t][:])
+
+        def m_on_vector(t):
+            nc.vector.tensor_copy(m_dst[t][:].indirect(offsets[:]), m_new[t][:])
+            nc.sync.dma_start(planes_of(out_1)[t], m_dst[t][:])
+
+        w_for_scalar(0)
+        w_on_scalar(0)
+        w_for_vector(1)
+        w_on_vector(1)
+        gather_m(2)
+        w_for_scalar(2)
+        nc.scalar.activation(m_dst[0][:, T // 2:], m_src[0][:, T // 2:], COPY)
+        nc.scalar.activation(m_dst[2][:], m_src[2][:], COPY)
+        w_on_scalar(2)
+        nc.vector.tensor_scalar(m_got[3][:], m_src[3][:].indirect(offsets[:]), M_IN_W, 0.0, MULT, ADD)
+        w_for_vector(3)
+        m_sum(0)
+        w_on_vector(3)
+        m_on_scalar(0)
+        m_sum(2)
+        m_on_scalar(2)
+        m_sum(1)
+        m_on_vector(1)
+        m_sum(3)
+        m_on_scalar(3)
+
+        words = out_2[0].rearrange("p c l -> p (c l)").bitcast(I32)
+        o_pairs = [keep.tile([P, 2, 2 * 512], BF16, name="o_pairs%d" % k, tag=("ym1", "rw3", "ym2", "ym3")[k])
+                   for k in range(T // 512)]
+
+        def round_planes(k, lo, hi, on_scalar):
+            for t in range(PACK):
+                dst = o_pairs[k][:, t // 2, :].rearrange("p (c e) -> p c e", e=2)[:, lo:hi, t % 2]
+                src = w_dst[t][:, 512 * k + lo:512 * k + hi]
+                if on_scalar:
+                    nc.scalar.activation(dst, src, COPY)
+                else:
+                    nc.vector.tensor_copy(dst, src)
+
+        round_planes(2, 256, 512, True)
+        round_planes(3, 0, 512, True)
+        o_w = [stage("o_w%d" % k) for k in range(T // 512)]
+
+        def weave_out(k):
+            nc.vector.tensor_copy(o_w[k][:].bitcast(F32).rearrange("p (c u) -> p c u", u=2),
+                                  o_pairs[k][:].bitcast(F32).rearrange("p u c -> p c u"))
+
+        def emit(k):
+            cols = slice(512 * k, 512 * (k + 1))
+            quantize(o_q, o_w[k][:], E4M3, cols)
+            nc.sync.dma_start(words[:, cols], o_q[0][:, cols].bitcast(I32))
+
+        round_planes(0, 0, 512, False)
+        weave_out(0)
+        round_planes(1, 0, 512, False)
+        emit(0)
+        weave_out(1)
+        round_planes(2, 0, 256, False)
+        emit(1)
+        weave_out(2)
+        weave_out(3)
+        emit(2)
+        emit(3)
+        for q in range(4):
+            nc.sync.dma_start(out_3[0][4 * q:4 * q + 4, :].bitcast(I32), o_q[1][32 * q:32 * q + 4, :].bitcast(I32))

@@ -40,14 +40,14 @@ def tile_attend_glch_pl_nag_kernel(tc, xT, wT, y, wt, xm, mT, offs, out_0, out_1
         w_src = [keep.tile([P, T], F32, name="w_src%d" % t) for t in range(PACK)]
         w_dst = [keep.tile([P, T], F32, name="w_dst%d" % t) for t in range(PACK)]
         m_src = [keep.tile([P, T], F32, name="m_src%d" % t) for t in range(PACK)]
-        m_dst = [keep.tile([P, T], F32, name="m_dst%d" % t) for t in range(PACK)]
-        x_raw = keep.tile([P, PACK, R], F32, name="x_raw")
+        m_dst = {t: keep.tile([P, T], F32, name="m_dst%d" % t) for t in (0, 1, 3)}
+        x_raw = [keep.tile([P, PACK, R // 2], F32, name="x_raw%d" % h) for h in range(2)]
         xm_raw = keep.tile([P, PACK, D], F32, name="xm_raw")
-        y_sb = [keep.tile([P, N], F32, name="y%d" % t, tag="ym%d" % t) for t in range(PACK)]
+        y_sb = [keep.tile([P, N], F32, name="y%d" % t, tag="ym%d" % t, align_bytes=64) for t in range(PACK)]
         wt_sb = keep.tile([P, PACK], F32, name="wt_sb")
-        w_got = keep.tile([P, PACK, N], F32, name="w_got", tag="wm")
+        w_got = keep.tile([P, PACK, N], F32, name="w_got", tag="wm", align_bytes=64)
         m_got = [keep.tile([P, N], F32, name="m_got%d" % t) for t in range(PACK)]
-        resid = [keep.tile([P, N], F32, name="resid%d" % t, tag="rw%d" % t) for t in range(PACK)]
+        resid = [keep.tile([P, N], F32, name="resid%d" % t, tag="rw%d" % t, align_bytes=64) for t in range(PACK)]
 
         def codes_and_scales(name, width):
             return (keep.tile([P, width], U32, name=name + "_codes", align_bytes=64),
@@ -65,11 +65,14 @@ def tile_attend_glch_pl_nag_kernel(tc, xT, wT, y, wt, xm, mT, offs, out_0, out_1
         def quantize(q, src, fmt, cols=slice(None)):
             nc.vector.quantize_mx(out=q[0][:, cols].bitcast(fmt), scales=q[1][:, cols], in_=src)
 
-        def deal(raw, dst):
-            out_v = dst[:].rearrange("p (t m j) -> p m j t", t=PACK, j=PACK)
-            in_v = raw[:].rearrange("p j (m t) -> p m j t", t=PACK)
-            nc.scalar.activation(out_v[:, :P // 2], in_v[:, :P // 2], COPY)
-            nc.vector.tensor_copy(out_v[:, P // 2:], in_v[:, P // 2:])
+        def dealt(dst):
+            return dst[:].rearrange("p (t m j) -> p m j t", t=PACK, j=PACK)
+
+        def undealt(raw):
+            return raw[:].rearrange("p j (m t) -> p m j t", t=PACK)
+
+        def quantize_block(q, src, t):
+            quantize(q, src[:, t * PACK * P:(t + 1) * PACK * P], E4M3, slice(t * P, (t + 1) * P))
 
         def weave_views(dst, src):
             return (dst.rearrange("p (c i t) -> p c t i", i=4, t=PACK),
@@ -78,7 +81,8 @@ def tile_attend_glch_pl_nag_kernel(tc, xT, wT, y, wt, xm, mT, offs, out_0, out_1
         nc.sync.dma_start(offsets[:], offs)
         for t in range(PACK):
             nc.sync.dma_start(w_src[t][:], planes_of(wT)[t])
-        nc.sync.dma_start(x_raw[:], xT[0].rearrange("(p j) r -> p j r", j=PACK))
+        for h in range(2):
+            nc.sync.dma_start(x_raw[h][:], xT[0].rearrange("(p j) r -> p j r", j=PACK)[:, :, 256 * h:256 * (h + 1)])
         nc.sync.dma_start(xm_raw[:], xm[0].rearrange("(p j) d -> p j d", j=PACK))
         for r in range(PACK):
             nc.sync.dma_start(y_sb[r][:], planes_of(y[0])[r])
@@ -90,21 +94,25 @@ def tile_attend_glch_pl_nag_kernel(tc, xT, wT, y, wt, xm, mT, offs, out_0, out_1
 
         def gather_w(t):
             nc.vector.tensor_copy(w_got[:, t, :], w_src[t][:].indirect(offsets[:]))
-            nc.scalar.activation(w_dst[t][:], w_src[t][:], COPY)
 
         def gather_m(t):
             nc.scalar.activation(m_got[t][:], m_src[t][:].indirect(offsets[:]), COPY, scale=M_IN_W)
 
         for t in range(PACK):
             gather_w(t)
+            width = T if t + 1 < PACK else T // 2
+            nc.scalar.activation(w_dst[t][:, :width], w_src[t][:, :width], COPY)
         w_w = stage("w_w")
         nc.vector.tensor_copy(*weave_views(w_w[:], w_got[:]))
         quantize(w_q, w_w[:], E4M3)
         x_w = stage("x_w")
-        deal(x_raw, x_w)
-        quantize(x_q, x_w[:], E4M3)
+        nc.scalar.activation(dealt(x_w)[:, :64], undealt(x_raw[0]), COPY)
+        nc.vector.tensor_copy(dealt(x_w)[:, 64:], undealt(x_raw[1]))
+        for r in range(PACK):
+            quantize_block(x_q, x_w, r)
+        nc.scalar.activation(w_dst[PACK - 1][:, T // 2:], w_src[PACK - 1][:, T // 2:], COPY)
         xm_w = stage("xm_w")
-        deal(xm_raw, xm_w)
+        nc.scalar.activation(dealt(xm_w), undealt(xm_raw), COPY)
 
         for r in range(PACK):
             score = psum.tile([P, N], F32, name="score%d" % r)
@@ -120,115 +128,101 @@ def tile_attend_glch_pl_nag_kernel(tc, xT, wT, y, wt, xm, mT, offs, out_0, out_1
         g_w = stage("g_w")
         nc.vector.tensor_copy(g_w[:].bitcast(F32).rearrange("p (i u) -> p i u", u=2),
                               g_pairs[:].bitcast(F32).rearrange("p (u i) -> p i u", u=2))
-        quantize(xm_q, xm_w[:, :PACK * P], E4M3, slice(0, P))
+        quantize_block(xm_q, xm_w, 0)
         quantize(g_q, g_w[:], E5M2)
         for t in range(1, PACK):
-            quantize(xm_q, xm_w[:, t * PACK * P:(t + 1) * PACK * P], E4M3, slice(t * P, (t + 1) * P))
+            quantize_block(xm_q, xm_w, t)
 
         gather_m(0)
         nc.scalar.activation(m_dst[0][:, :T // 2], m_src[0][:, :T // 2], COPY)
         gather_m(1)
 
         dw = []
-        for t in range(PACK):
+
+        def gradient(t):
             bank = psum.tile([P, N], F32, name="dw%d" % t)
             cols = slice(t * P, (t + 1) * P)
             nc.tensor.matmul_mx(out=bank[:], lhsT=xm_q[0][:, cols].bitcast(E4M3), lhsT_scale=xm_q[1][:, cols],
                                 rhs=g_q[0][:].bitcast(E5M2), rhs_scale=g_q[1][:], start=True, stop=True)
             dw.append(bank)
 
-        w_part = [keep.tile([P, N], F32, name="w_part%d" % t, tag="rw%d" % t) for t in range(PACK)]
-        m_new = [keep.tile([P, N], F32, name="m_new%d" % t, tag="ym%d" % t if t else "wm") for t in range(PACK)]
+        w_new = [keep.tile([P, N], F32, name="w_new%d" % t, tag="rw%d" % t, align_bytes=64) for t in range(PACK)]
+        m_new = [keep.tile([P, N], F32, name="m_new%d" % t, tag=("wm", "rw3", "ym2", "ym3")[t], align_bytes=64) for t in range(PACK)]
+        m_dst[2] = keep.tile([P, T], F32, name="m_dst2", tag="rw2", align_bytes=64)
+        o_pairs = [keep.tile([P, 2, 2 * 512], BF16, name="o_pairs%d" % k) for k in range(T // 512)]
 
-        def scatter_on_scalar(window, values):
+        def scatter(window, values, halves_on_scalar):
+            if halves_on_scalar == 0:
+                nc.vector.tensor_copy(window[:].indirect(offsets[:]), values[:])
+                return
             for h in range(2):
-                nc.scalar.activation(window[:].indirect(offsets[:, 16 * h:16 * (h + 1)]),
-                                     values[:, 256 * h:256 * (h + 1)], COPY)
+                target = window[:].indirect(offsets[:, 16 * h:16 * (h + 1)])
+                if h >= 2 - halves_on_scalar:
+                    nc.scalar.activation(target, values[:, 256 * h:256 * (h + 1)], COPY)
+                else:
+                    nc.vector.tensor_copy(target, values[:, 256 * h:256 * (h + 1)])
 
-        def w_for_scalar(t):
-            nc.vector.tensor_tensor(w_part[t][:], w_got[:, t, :], m_got[t][:], ADD)
-            nc.vector.scalar_tensor_tensor(w_part[t][:], dw[t][:], DW_IN_W, w_part[t][:], MULT, ADD)
+        def w_base(t):
+            nc.vector.tensor_tensor(w_new[t][:], w_got[:, t, :], m_got[t][:], ADD)
 
-        def w_on_scalar(t):
-            scatter_on_scalar(w_dst[t], w_part[t])
+        def w_sum(t):
+            nc.vector.scalar_tensor_tensor(w_new[t][:], dw[t][:], DW_IN_W, w_new[t][:], MULT, ADD)
+
+        def w_out(t):
+            scatter(w_dst[t], w_new[t], 2 if t % 2 == 0 else 0)
             nc.sync.dma_start(planes_of(out_0)[t], w_dst[t][:])
-
-        def w_for_vector(t):
-            nc.vector.scalar_tensor_tensor(w_part[t][:], dw[t][:], DW_IN_W, w_got[:, t, :], MULT, ADD)
-
-        def w_on_vector(t):
-            nc.vector.tensor_tensor(w_dst[t][:].indirect(offsets[:]), w_part[t][:], m_got[t][:], ADD)
-            nc.sync.dma_start(planes_of(out_0)[t], w_dst[t][:])
+            for k in range(T // 512):
+                nc.gpsimd.tensor_scalar(o_pairs[k][:, t // 2, :].rearrange("p (c e) -> p c e", e=2)[:, :, t % 2],
+                                        w_dst[t][:, 512 * k:512 * (k + 1)], 1.0, -0.0, MULT, ADD)
 
         def m_sum(t):
             nc.vector.scalar_tensor_tensor(m_new[t][:], m_got[t][:], BETA / M_IN_W, dw[t][:], MULT, ADD)
 
-        def m_on_scalar(t):
-            scatter_on_scalar(m_dst[t], m_new[t])
+        def m_out(t):
+            scatter(m_dst[t], m_new[t], 1 if t == 1 else 2)
             queue = nc.scalar if t == PACK - 1 else nc.sync
             queue.dma_start(planes_of(out_1)[t], m_dst[t][:])
 
-        def m_on_vector(t):
-            nc.vector.tensor_copy(m_dst[t][:].indirect(offsets[:]), m_new[t][:])
-            nc.sync.dma_start(planes_of(out_1)[t], m_dst[t][:])
-
-        w_for_scalar(0)
-        w_on_scalar(0)
-        w_for_vector(1)
-        w_on_vector(1)
+        for t in range(PACK):
+            gradient(t)
+        w_base(0)
+        w_sum(0)
+        w_out(0)
+        w_base(1)
+        w_sum(1)
+        w_out(1)
         gather_m(2)
-        w_for_scalar(2)
         nc.scalar.activation(m_dst[0][:, T // 2:], m_src[0][:, T // 2:], COPY)
-        nc.scalar.activation(m_dst[2][:], m_src[2][:], COPY)
-        w_on_scalar(2)
+        w_base(2)
+        w_sum(2)
+        w_out(2)
         nc.vector.tensor_scalar(m_got[3][:], m_src[3][:].indirect(offsets[:]), M_IN_W, 0.0, MULT, ADD)
-        w_for_vector(3)
+        w_base(3)
         m_sum(0)
-        w_on_vector(3)
-        m_on_scalar(0)
+        w_sum(3)
+        w_out(3)
+        m_out(0)
+        nc.scalar.activation(m_dst[2][:], m_src[2][:], COPY)
         m_sum(2)
-        m_on_scalar(2)
         m_sum(1)
-        m_on_vector(1)
+        m_out(2)
+        m_out(1)
         m_sum(3)
-        m_on_scalar(3)
+        m_out(3)
 
         words = out_2[0].rearrange("p c l -> p (c l)").bitcast(I32)
-        o_pairs = [keep.tile([P, 2, 2 * 512], BF16, name="o_pairs%d" % k, tag=("ym1", "rw3", "ym2", "ym3")[k])
-                   for k in range(T // 512)]
-
-        def round_planes(k, lo, hi, on_scalar):
-            for t in range(PACK):
-                dst = o_pairs[k][:, t // 2, :].rearrange("p (c e) -> p c e", e=2)[:, lo:hi, t % 2]
-                src = w_dst[t][:, 512 * k + lo:512 * k + hi]
-                if on_scalar:
-                    nc.scalar.activation(dst, src, COPY)
-                else:
-                    nc.vector.tensor_copy(dst, src)
-
-        round_planes(2, 256, 512, True)
-        round_planes(3, 0, 512, True)
         o_w = [stage("o_w%d" % k) for k in range(T // 512)]
 
         def weave_out(k):
             nc.vector.tensor_copy(o_w[k][:].bitcast(F32).rearrange("p (c u) -> p c u", u=2),
                                   o_pairs[k][:].bitcast(F32).rearrange("p u c -> p c u"))
 
-        def emit(k):
+        weave_out(0)
+        for k in range(T // 512):
             cols = slice(512 * k, 512 * (k + 1))
+            if k + 1 < T // 512:
+                weave_out(k + 1)
             quantize(o_q, o_w[k][:], E4M3, cols)
             nc.sync.dma_start(words[:, cols], o_q[0][:, cols].bitcast(I32))
-
-        round_planes(0, 0, 512, False)
-        weave_out(0)
-        round_planes(1, 0, 512, False)
-        emit(0)
-        weave_out(1)
-        round_planes(2, 0, 256, False)
-        emit(1)
-        weave_out(2)
-        weave_out(3)
-        emit(2)
-        emit(3)
         for q in range(4):
             nc.sync.dma_start(out_3[0][4 * q:4 * q + 4, :].bitcast(I32), o_q[1][32 * q:32 * q + 4, :].bitcast(I32))

@@ -30,7 +30,7 @@ def tile_attend_glch_pl_nag_kernel(tc, xT, wT, y, wt, xm, mT, offs, out_0, out_1
     nc = tc.nc
     with ExitStack() as ctx:
         keep = ctx.enter_context(tc.tile_pool(name="keep", bufs=1))
-        woven = ctx.enter_context(tc.tile_pool(name="woven", bufs=5))
+        woven = ctx.enter_context(tc.tile_pool(name="woven", bufs=4))
         psum = ctx.enter_context(tc.psum_pool(name="psum", bufs=1))
 
         def planes_of(table):
@@ -40,13 +40,13 @@ def tile_attend_glch_pl_nag_kernel(tc, xT, wT, y, wt, xm, mT, offs, out_0, out_1
         w_src = [keep.tile([P, T], F32, name="w_src%d" % t) for t in range(PACK)]
         w_dst = [keep.tile([P, T], F32, name="w_dst%d" % t) for t in range(PACK)]
         m_src = [keep.tile([P, T], F32, name="m_src%d" % t) for t in range(PACK)]
-        m_dst = {t: keep.tile([P, T], F32, name="m_dst%d" % t) for t in (0, 1, 3)}
+        m_dst = [keep.tile([P, T], F32, name="m_dst%d" % t) for t in range(PACK)]
         x_raw = [keep.tile([P, PACK, R // 2], F32, name="x_raw%d" % h) for h in range(2)]
-        xm_raw = keep.tile([P, PACK, D], F32, name="xm_raw")
+        xm_raw = keep.tile([P, PACK, D], F32, name="xm_raw", tag="rw0", align_bytes=64)
         y_sb = [keep.tile([P, N], F32, name="y%d" % t, tag="ym%d" % t, align_bytes=64) for t in range(PACK)]
         wt_sb = keep.tile([P, PACK], F32, name="wt_sb")
         w_got = keep.tile([P, PACK, N], F32, name="w_got", tag="wm", align_bytes=64)
-        m_got = [keep.tile([P, N], F32, name="m_got%d" % t) for t in range(PACK)]
+        m_got = [keep.tile([P, N], F32, name="m_got%d" % t, tag="m_got%d" % t, align_bytes=64) for t in range(PACK)]
         resid = [keep.tile([P, N], F32, name="resid%d" % t, tag="rw%d" % t, align_bytes=64) for t in range(PACK)]
 
         def codes_and_scales(name, width):
@@ -89,11 +89,15 @@ def tile_attend_glch_pl_nag_kernel(tc, xT, wT, y, wt, xm, mT, offs, out_0, out_1
         nc.sync.dma_start(wt_sb[:], wt[0].rearrange("(p j) o -> p (j o)", j=PACK))
         for t in range(PACK):
             nc.sync.dma_start(m_src[t][:], planes_of(mT)[t])
-        for t in (1, 3):
+        for t in range(1, PACK):
             nc.sync.dma_start(m_dst[t][:], planes_of(mT)[t])
 
         def gather_w(t):
-            nc.vector.tensor_copy(w_got[:, t, :], w_src[t][:].indirect(offsets[:]))
+            if t + 1 < PACK:
+                nc.vector.tensor_copy(w_got[:, t, :], w_src[t][:].indirect(offsets[:]))
+            else:
+                nc.vector.tensor_copy(w_got[:, t, :256], w_src[t][:].indirect(offsets[:, :16]))
+                nc.scalar.activation(w_got[:, t, 256:], w_src[t][:].indirect(offsets[:, 16:]), COPY)
 
         def gather_m(t):
             nc.scalar.activation(m_got[t][:], m_src[t][:].indirect(offsets[:]), COPY, scale=M_IN_W)
@@ -112,7 +116,8 @@ def tile_attend_glch_pl_nag_kernel(tc, xT, wT, y, wt, xm, mT, offs, out_0, out_1
             quantize_block(x_q, x_w, r)
         nc.scalar.activation(w_dst[PACK - 1][:, T // 2:], w_src[PACK - 1][:, T // 2:], COPY)
         xm_w = stage("xm_w")
-        nc.scalar.activation(dealt(xm_w), undealt(xm_raw), COPY)
+        nc.scalar.activation(dealt(xm_w)[:, :64], undealt(xm_raw)[:, :64], COPY)
+        nc.vector.tensor_copy(dealt(xm_w)[:, 64:], undealt(xm_raw)[:, 64:])
 
         for r in range(PACK):
             score = psum.tile([P, N], F32, name="score%d" % r)
@@ -136,6 +141,7 @@ def tile_attend_glch_pl_nag_kernel(tc, xT, wT, y, wt, xm, mT, offs, out_0, out_1
         gather_m(0)
         nc.scalar.activation(m_dst[0][:, :T // 2], m_src[0][:, :T // 2], COPY)
         gather_m(1)
+        nc.scalar.activation(m_dst[0][:, T // 2:], m_src[0][:, T // 2:], COPY)
 
         dw = []
 
@@ -146,83 +152,91 @@ def tile_attend_glch_pl_nag_kernel(tc, xT, wT, y, wt, xm, mT, offs, out_0, out_1
                                 rhs=g_q[0][:].bitcast(E5M2), rhs_scale=g_q[1][:], start=True, stop=True)
             dw.append(bank)
 
-        w_new = [keep.tile([P, N], F32, name="w_new%d" % t, tag="rw%d" % t, align_bytes=64) for t in range(PACK)]
-        m_new = [keep.tile([P, N], F32, name="m_new%d" % t, tag=("wm", "rw3", "ym2", "ym3")[t], align_bytes=64) for t in range(PACK)]
-        m_dst[2] = keep.tile([P, T], F32, name="m_dst2", tag="rw2", align_bytes=64)
-        o_pairs = [keep.tile([P, 2, 2 * 512], BF16, name="o_pairs%d" % k) for k in range(T // 512)]
+        def shared(name, tag, shape=(P, N), dtype=F32):
+            return keep.tile(list(shape), dtype, name=name, tag=tag, align_bytes=64)
 
-        def scatter(window, values, halves_on_scalar):
-            if halves_on_scalar == 0:
-                nc.vector.tensor_copy(window[:].indirect(offsets[:]), values[:])
-                return
+        w_base = {t: shared("w_base%d" % t, "rw3") for t in (0, 2)}
+        w_new = [shared("w_new%d" % t, ("rw0", "rw3", "rw2", "rw3")[t]) for t in range(PACK)]
+        m_new = [shared("m_new%d" % t, "ym%d" % t) for t in range(PACK)]
+        o_pairs = [shared("o_pairs%d" % h, ("m_got3", "rw3")[h], (P, 2, T), BF16) for h in range(2)]
+
+        def gather_m_on_vector(t):
+            nc.vector.tensor_scalar(m_got[t][:], m_src[t][:].indirect(offsets[:]), M_IN_W, 0.0, MULT, ADD)
+
+        def scatter_on_scalar(window, values):
             for h in range(2):
-                target = window[:].indirect(offsets[:, 16 * h:16 * (h + 1)])
-                if h >= 2 - halves_on_scalar:
-                    nc.scalar.activation(target, values[:, 256 * h:256 * (h + 1)], COPY)
-                else:
-                    nc.vector.tensor_copy(target, values[:, 256 * h:256 * (h + 1)])
+                nc.scalar.activation(window[:].indirect(offsets[:, 16 * h:16 * (h + 1)]),
+                                     values[:, 256 * h:256 * (h + 1)], COPY)
 
-        def w_base(t):
-            nc.vector.tensor_tensor(w_new[t][:], w_got[:, t, :], m_got[t][:], ADD)
+        def w_whole(t):
+            nc.vector.tensor_tensor(w_base[t][:], w_got[:, t, :], m_got[t][:], ADD)
+            nc.vector.scalar_tensor_tensor(w_new[t][:], dw[t][:], DW_IN_W, w_base[t][:], MULT, ADD)
 
-        def w_sum(t):
-            nc.vector.scalar_tensor_tensor(w_new[t][:], dw[t][:], DW_IN_W, w_new[t][:], MULT, ADD)
-
-        def w_out(t):
-            scatter(w_dst[t], w_new[t], 2 if t % 2 == 0 else 0)
+        def w_on_scalar(t):
+            scatter_on_scalar(w_dst[t], w_new[t])
             nc.sync.dma_start(planes_of(out_0)[t], w_dst[t][:])
-            for k in range(T // 512):
-                nc.gpsimd.tensor_scalar(o_pairs[k][:, t // 2, :].rearrange("p (c e) -> p c e", e=2)[:, :, t % 2],
-                                        w_dst[t][:, 512 * k:512 * (k + 1)], 1.0, -0.0, MULT, ADD)
+
+        def w_part(t):
+            nc.vector.scalar_tensor_tensor(w_new[t][:], dw[t][:], DW_IN_W, w_got[:, t, :], MULT, ADD)
+
+        def w_on_vector(t):
+            nc.vector.tensor_tensor(w_dst[t][:].indirect(offsets[:]), w_new[t][:], m_got[t][:], ADD)
+            nc.sync.dma_start(planes_of(out_0)[t], w_dst[t][:])
 
         def m_sum(t):
             nc.vector.scalar_tensor_tensor(m_new[t][:], m_got[t][:], BETA / M_IN_W, dw[t][:], MULT, ADD)
 
         def m_out(t):
-            scatter(m_dst[t], m_new[t], 1 if t == 1 else 2)
-            queue = nc.scalar if t == PACK - 1 else nc.sync
-            queue.dma_start(planes_of(out_1)[t], m_dst[t][:])
+            scatter_on_scalar(m_dst[t], m_new[t])
+            nc.sync.dma_start(planes_of(out_1)[t], m_dst[t][:])
+
+        def round_plane(t, h):
+            nc.vector.tensor_copy(o_pairs[h][:, t // 2, :].rearrange("p (c e) -> p c e", e=2)[:, :, t % 2],
+                                  w_dst[t][:, h * T // 2:(h + 1) * T // 2])
 
         for t in range(PACK):
             gradient(t)
-        w_base(0)
-        w_sum(0)
-        w_out(0)
-        w_base(1)
-        w_sum(1)
-        w_out(1)
-        gather_m(2)
-        nc.scalar.activation(m_dst[0][:, T // 2:], m_src[0][:, T // 2:], COPY)
-        w_base(2)
-        w_sum(2)
-        w_out(2)
-        nc.vector.tensor_scalar(m_got[3][:], m_src[3][:].indirect(offsets[:]), M_IN_W, 0.0, MULT, ADD)
-        w_base(3)
+        w_whole(0)
+        w_on_scalar(0)
         m_sum(0)
-        w_sum(3)
-        w_out(3)
+        gather_m_on_vector(2)
+        w_whole(2)
+        w_on_scalar(2)
         m_out(0)
-        nc.scalar.activation(m_dst[2][:], m_src[2][:], COPY)
-        m_sum(2)
+        w_part(1)
         m_sum(1)
-        m_out(2)
         m_out(1)
+        w_on_vector(1)
+        gather_m_on_vector(3)
+        w_part(3)
+        m_sum(2)
+        m_out(2)
+        w_on_vector(3)
         m_sum(3)
         m_out(3)
+        for h in (1, 0):
+            for t in range(PACK):
+                round_plane(t, h)
 
         words = out_2[0].rearrange("p c l -> p (c l)").bitcast(I32)
-        o_w = [stage("o_w%d" % k) for k in range(T // 512)]
+        o_w = [shared("o_w%d" % h, ("ym2", "ym3")[h], (P, PACK * T // 2), BF16) for h in range(2)]
+
+        def chunk(k):
+            return o_w[k // 2][:, PACK * 512 * (k % 2):PACK * 512 * (k % 2 + 1)]
 
         def weave_out(k):
-            nc.vector.tensor_copy(o_w[k][:].bitcast(F32).rearrange("p (c u) -> p c u", u=2),
-                                  o_pairs[k][:].bitcast(F32).rearrange("p u c -> p c u"))
+            move = nc.scalar.copy if k >= 2 else nc.vector.tensor_copy
+            move(chunk(k).bitcast(F32).rearrange("p (c u) -> p c u", u=2),
+                 o_pairs[k // 2][:].bitcast(F32)[:, :, 512 * (k % 2):512 * (k % 2 + 1)].rearrange("p u c -> p c u"))
 
-        weave_out(0)
-        for k in range(T // 512):
+        def emit(k):
             cols = slice(512 * k, 512 * (k + 1))
-            if k + 1 < T // 512:
-                weave_out(k + 1)
-            quantize(o_q, o_w[k][:], E4M3, cols)
+            quantize(o_q, chunk(k), E4M3, cols)
             nc.sync.dma_start(words[:, cols], o_q[0][:, cols].bitcast(I32))
+
+        for k in range(T // 512):
+            weave_out(k)
+        for k in range(T // 512):
+            emit(k)
         for q in range(4):
             nc.sync.dma_start(out_3[0][4 * q:4 * q + 4, :].bitcast(I32), o_q[1][32 * q:32 * q + 4, :].bitcast(I32))

@@ -78,8 +78,9 @@ def tile_attend_glch_pl_nag_kernel(tc, xT, wT, y, wt, xm, mT, offs, out_0, out_1
             return (dst.rearrange("p (c i t) -> p c t i", i=4, t=PACK),
                     src.rearrange("p t (c i) -> p c t i", i=4))
 
+        nc.sync.dma_start(w_src[0][:], planes_of(wT)[0])
         nc.sync.dma_start(offsets[:], offs)
-        for t in range(PACK):
+        for t in range(1, PACK):
             nc.sync.dma_start(w_src[t][:], planes_of(wT)[t])
         for h in range(2):
             nc.sync.dma_start(x_raw[h][:], xT[0].rearrange("(p j) r -> p j r", j=PACK)[:, :, 256 * h:256 * (h + 1)])
@@ -174,7 +175,8 @@ def tile_attend_glch_pl_nag_kernel(tc, xT, wT, y, wt, xm, mT, offs, out_0, out_1
 
         def w_on_scalar(t):
             scatter_on_scalar(w_dst[t], w_new[t])
-            nc.sync.dma_start(planes_of(out_0)[t], w_dst[t][:])
+            queue = nc.scalar if t == 2 else nc.sync
+            queue.dma_start(planes_of(out_0)[t], w_dst[t][:])
 
         def w_part(t):
             nc.vector.scalar_tensor_tensor(w_new[t][:], dw[t][:], DW_IN_W, w_got[:, t, :], MULT, ADD)
@@ -232,7 +234,9 @@ def tile_attend_glch_pl_nag_kernel(tc, xT, wT, y, wt, xm, mT, offs, out_0, out_1
         def emit(k):
             cols = slice(512 * k, 512 * (k + 1))
             quantize(o_q, chunk(k), E4M3, cols)
-            nc.sync.dma_start(words[:, cols], o_q[0][:, cols].bitcast(I32))
+            if k > 0:
+                done = slice(0, 1024) if k == 1 else cols
+                nc.sync.dma_start(words[:, done], o_q[0][:, done].bitcast(I32))
 
         for k in range(T // 512):
             weave_out(k)

from contextlib import ExitStack

import concourse.mybir as mybir

D, R, N, T = 512, 512, 512, 2048
LR, BETA = 0.1, 0.9
FLOPS = 2 * 2 * D * R * N

F32 = mybir.dt.float32
BF16 = mybir.dt.bfloat16
I32 = mybir.dt.int32
U32 = mybir.dt.uint32
U16 = mybir.dt.uint16
U8 = mybir.dt.uint8
E4M3 = mybir.dt.float8_e4m3fn_x4
E5M2 = mybir.dt.float8_e5m2_x4
COPY = mybir.ActivationFunctionType.Copy
TANH = mybir.ActivationFunctionType.Tanh
MULT = mybir.AluOpType.mult
ADD = mybir.AluOpType.add
SUB = mybir.AluOpType.subtract

P = 128
PACK = 4
M_IN_W = -LR * BETA * BETA
DW_IN_W = -LR * (1.0 + BETA)


def tile_attend_glch_pl_nag_kernel(tc, xT, wT, y, wt, xm, mT, offs, out_0, out_1, out_2, out_3):
    nc = tc.nc
    with ExitStack() as ctx:
        keep = ctx.enter_context(tc.tile_pool(name="keep", bufs=1))
        woven = ctx.enter_context(tc.tile_pool(name="woven", bufs=4))
        psum = ctx.enter_context(tc.psum_pool(name="psum", bufs=1))

        def planes_of(table):
            return table.rearrange("(p t) c -> t p c", t=PACK)

        offsets = keep.tile([P, N // 16], U16, name="offsets")
        w_src = [keep.tile([P, T], F32, name="w_src%d" % t) for t in range(PACK)]
        w_dst = [keep.tile([P, T], F32, name="w_dst%d" % t) for t in range(PACK)]
        m_src = [keep.tile([P, T], F32, name="m_src%d" % t) for t in range(PACK)]
        m_dst = [keep.tile([P, T], F32, name="m_dst%d" % t) for t in range(PACK)]
        x_raw = [keep.tile([P, PACK, R // 2], F32, name="x_raw%d" % h) for h in range(2)]
        xm_raw = keep.tile([P, PACK, D], F32, name="xm_raw", tag="rw0", align_bytes=64)
        y_sb = [keep.tile([P, N], F32, name="y%d" % t, tag="ym%d" % t, align_bytes=64) for t in range(PACK)]
        wt_sb = keep.tile([P, PACK], F32, name="wt_sb")
        w_got = keep.tile([P, PACK, N], F32, name="w_got", tag="wm", align_bytes=64)
        m_got = [keep.tile([P, N], F32, name="m_got%d" % t, tag="m_got%d" % t, align_bytes=64) for t in range(PACK)]
        resid = [keep.tile([P, N], F32, name="resid%d" % t, tag="rw%d" % t, align_bytes=64) for t in range(PACK)]

        def codes_and_scales(name, width):
            return (keep.tile([P, width], U32, name=name + "_codes", align_bytes=64),
                    keep.tile([P, width], U8, name=name + "_scales", align_bytes=64))

        x_q = codes_and_scales("x", R)
        w_q = codes_and_scales("w", N)
        xm_q = codes_and_scales("xm", D)
        g_q = codes_and_scales("g", N)
        o_q = codes_and_scales("o", T)

        def stage(name):
            return woven.tile([P, PACK * 512], BF16, name=name, tag="woven", align_bytes=64)

        def quantize(q, src, fmt, cols=slice(None)):
            nc.vector.quantize_mx(out=q[0][:, cols].bitcast(fmt), scales=q[1][:, cols], in_=src)

        def dealt(dst):
            return dst[:].rearrange("p (t m j) -> p m j t", t=PACK, j=PACK)

        def undealt(raw):
            return raw[:].rearrange("p j (m t) -> p m j t", t=PACK)

        def quantize_block(q, src, t):
            quantize(q, src[:, t * PACK * P:(t + 1) * PACK * P], E4M3, slice(t * P, (t + 1) * P))

        def weave_views(dst, src):
            return (dst.rearrange("p (c i t) -> p c t i", i=4, t=PACK),
                    src.rearrange("p t (c i) -> p c t i", i=4))

        nc.sync.dma_start(w_src[0][:], planes_of(wT)[0])
        nc.sync.dma_start(offsets[:], offs)
        for t in range(1, PACK):
            nc.sync.dma_start(w_src[t][:], planes_of(wT)[t])
        for h in range(2):
            nc.sync.dma_start(x_raw[h][:], xT[0].rearrange("(p j) r -> p j r", j=PACK)[:, :, 256 * h:256 * (h + 1)])
        nc.sync.dma_start(xm_raw[:], xm[0].rearrange("(p j) d -> p j d", j=PACK))
        for r in range(PACK):
            nc.sync.dma_start(y_sb[r][:], planes_of(y[0])[r])
        nc.sync.dma_start(wt_sb[:], wt[0].rearrange("(p j) o -> p (j o)", j=PACK))
        for t in range(PACK):
            nc.sync.dma_start(m_src[t][:], planes_of(mT)[t])
        for t in range(1, PACK):
            nc.sync.dma_start(m_dst[t][:], planes_of(mT)[t])

        def gather_w(t):
            if t + 1 < PACK:
                nc.vector.tensor_copy(w_got[:, t, :], w_src[t][:].indirect(offsets[:]))
            else:
                nc.vector.tensor_copy(w_got[:, t, :256], w_src[t][:].indirect(offsets[:, :16]))
                nc.scalar.activation(w_got[:, t, 256:], w_src[t][:].indirect(offsets[:, 16:]), COPY)

        def gather_m(t):
            nc.scalar.activation(m_got[t][:], m_src[t][:].indirect(offsets[:]), COPY, scale=M_IN_W)

        for t in range(PACK):
            gather_w(t)
            width = T if t + 1 < PACK else T // 2
            nc.scalar.activation(w_dst[t][:, :width], w_src[t][:, :width], COPY)
        w_w = stage("w_w")
        nc.vector.tensor_copy(*weave_views(w_w[:], w_got[:]))
        quantize(w_q, w_w[:], E4M3)
        x_w = stage("x_w")
        nc.scalar.activation(dealt(x_w)[:, :64], undealt(x_raw[0]), COPY)
        nc.vector.tensor_copy(dealt(x_w)[:, 64:], undealt(x_raw[1]))
        for r in range(PACK):
            quantize_block(x_q, x_w, r)
        nc.scalar.activation(w_dst[PACK - 1][:, T // 2:], w_src[PACK - 1][:, T // 2:], COPY)
        xm_w = stage("xm_w")
        nc.scalar.activation(dealt(xm_w)[:, :64], undealt(xm_raw)[:, :64], COPY)
        nc.vector.tensor_copy(dealt(xm_w)[:, 64:], undealt(xm_raw)[:, 64:])

        for r in range(PACK):
            score = psum.tile([P, N], F32, name="score%d" % r)
            cols = slice(r * P, (r + 1) * P)
            nc.tensor.matmul_mx(out=score[:], lhsT=x_q[0][:, cols].bitcast(E4M3), lhsT_scale=x_q[1][:, cols],
                                rhs=w_q[0][:].bitcast(E4M3), rhs_scale=w_q[1][:], start=True, stop=True)
            nc.vector.tensor_tensor(resid[r][:], score[:], y_sb[r][:], SUB)
            nc.scalar.activation(resid[r][:], resid[r][:], TANH)
        g_pairs = stage("g_pairs")
        g_half = g_pairs[:].rearrange("p (u i e) -> p u i e", u=2, e=2)
        for r in range(PACK):
            nc.vector.tensor_scalar(g_half[:, r // 2, :, r % 2], resid[r][:], wt_sb[:, r:r + 1], None, MULT)
        g_w = stage("g_w")
        nc.vector.tensor_copy(g_w[:].bitcast(F32).rearrange("p (i u) -> p i u", u=2),
                              g_pairs[:].bitcast(F32).rearrange("p (u i) -> p i u", u=2))
        quantize_block(xm_q, xm_w, 0)
        quantize(g_q, g_w[:], E5M2)
        for t in range(1, PACK):
            quantize_block(xm_q, xm_w, t)

        gather_m(0)
        nc.scalar.activation(m_dst[0][:, :T // 2], m_src[0][:, :T // 2], COPY)
        gather_m(1)
        nc.scalar.activation(m_dst[0][:, T // 2:], m_src[0][:, T // 2:], COPY)

        dw = []

        def gradient(t):
            bank = psum.tile([P, N], F32, name="dw%d" % t)
            cols = slice(t * P, (t + 1) * P)
            nc.tensor.matmul_mx(out=bank[:], lhsT=xm_q[0][:, cols].bitcast(E4M3), lhsT_scale=xm_q[1][:, cols],
                                rhs=g_q[0][:].bitcast(E5M2), rhs_scale=g_q[1][:], start=True, stop=True)
            dw.append(bank)

        def shared(name, tag, shape=(P, N), dtype=F32):
            return keep.tile(list(shape), dtype, name=name, tag=tag, align_bytes=64)

        w_base = {t: shared("w_base%d" % t, "rw3") for t in (0, 2)}
        w_new = [shared("w_new%d" % t, ("rw0", "rw3", "rw2", "rw3")[t]) for t in range(PACK)]
        m_new = [shared("m_new%d" % t, "ym%d" % t) for t in range(PACK)]
        o_pairs = [shared("o_pairs%d" % h, ("m_got3", "rw3")[h], (P, 2, T), BF16) for h in range(2)]

        def gather_m_on_vector(t):
            nc.vector.tensor_scalar(m_got[t][:], m_src[t][:].indirect(offsets[:]), M_IN_W, 0.0, MULT, ADD)

        def scatter_on_scalar(window, values):
            for h in range(2):
                nc.scalar.activation(window[:].indirect(offsets[:, 16 * h:16 * (h + 1)]),
                                     values[:, 256 * h:256 * (h + 1)], COPY)

        def w_whole(t):
            nc.vector.tensor_tensor(w_base[t][:], w_got[:, t, :], m_got[t][:], ADD)
            nc.vector.scalar_tensor_tensor(w_new[t][:], dw[t][:], DW_IN_W, w_base[t][:], MULT, ADD)

        def w_on_scalar(t):
            scatter_on_scalar(w_dst[t], w_new[t])
            queue = nc.scalar if t == 2 else nc.sync
            queue.dma_start(planes_of(out_0)[t], w_dst[t][:])

        def w_part(t):
            nc.vector.scalar_tensor_tensor(w_new[t][:], dw[t][:], DW_IN_W, w_got[:, t, :], MULT, ADD)

        def w_on_vector(t):
            nc.vector.tensor_tensor(w_dst[t][:].indirect(offsets[:]), w_new[t][:], m_got[t][:], ADD)
            nc.sync.dma_start(planes_of(out_0)[t], w_dst[t][:])

        def m_sum(t):
            nc.vector.scalar_tensor_tensor(m_new[t][:], m_got[t][:], BETA / M_IN_W, dw[t][:], MULT, ADD)

        def m_out(t):
            scatter_on_scalar(m_dst[t], m_new[t])
            nc.sync.dma_start(planes_of(out_1)[t], m_dst[t][:])

        def round_plane(t, h):
            nc.vector.tensor_copy(o_pairs[h][:, t // 2, :].rearrange("p (c e) -> p c e", e=2)[:, :, t % 2],
                                  w_dst[t][:, h * T // 2:(h + 1) * T // 2])

        for t in range(PACK):
            gradient(t)
        w_whole(0)
        w_on_scalar(0)
        m_sum(0)
        gather_m_on_vector(2)
        w_whole(2)
        w_on_scalar(2)
        m_out(0)
        w_part(1)
        m_sum(1)
        m_out(1)
        w_on_vector(1)
        gather_m_on_vector(3)
        w_part(3)
        m_sum(2)
        m_out(2)
        w_on_vector(3)
        m_sum(3)
        m_out(3)
        for h in (1, 0):
            for t in range(PACK):
                round_plane(t, h)

        words = out_2[0].rearrange("p c l -> p (c l)").bitcast(I32)
        o_w = [shared("o_w%d" % h, ("ym2", "ym3")[h], (P, PACK * T // 2), BF16) for h in range(2)]

        def chunk(k):
            return o_w[k // 2][:, PACK * 512 * (k % 2):PACK * 512 * (k % 2 + 1)]

        def weave_out(k):
            move = nc.scalar.copy if k >= 2 else nc.vector.tensor_copy
            move(chunk(k).bitcast(F32).rearrange("p (c u) -> p c u", u=2),
                 o_pairs[k // 2][:].bitcast(F32)[:, :, 512 * (k % 2):512 * (k % 2 + 1)].rearrange("p u c -> p c u"))

        def emit(k):
            cols = slice(512 * k, 512 * (k + 1))
            quantize(o_q, chunk(k), E4M3, cols)
            if k > 0:
                done = slice(0, 1024) if k == 1 else cols
                nc.sync.dma_start(words[:, done], o_q[0][:, done].bitcast(I32))

        for k in range(T // 512):
            weave_out(k)
        for k in range(T // 512):
            emit(k)
        for q in range(4):
            nc.sync.dma_start(out_3[0][4 * q:4 * q + 4, :].bitcast(I32), o_q[1][32 * q:32 * q + 4, :].bitcast(I32))
